import numpy as np
import ml_dtypes


def mxq(x, axis, fmt="e4m3"):
    dtype, down = {"e4m3": (ml_dtypes.float8_e4m3fn, 7), "e5m2": (ml_dtypes.float8_e5m2, 14)}[fmt]
    v = np.moveaxis(np.asarray(x, np.float32).astype(ml_dtypes.bfloat16).astype(np.float64), axis, -1)
    blocks = v.reshape(v.shape[:-1] + (-1, 32))
    amax = np.abs(blocks).max(-1, keepdims=True)
    byte = np.maximum(np.where(amax > 0, np.frexp(amax)[1] - 1 + 127, 0) - down, 1)
    scale = np.exp2(byte - 127.0)
    codes = (blocks / scale).astype(np.float32).astype(dtype).astype(np.float64)
    return np.moveaxis((codes * scale).reshape(v.shape), -1, axis)


WIDE = False


def mx_kscale(k):
    if not WIDE:
        return np.ones(k)
    levels = np.array([10, -10, 5, -5, 0])
    if k % 512:
        return np.exp2(np.random.permutation(np.resize(levels, k // 32))).repeat(32)
    a = np.empty((k // 512, 16))
    for p in range(k // 512):
        a[p, :8] = np.random.permutation(np.resize(levels, 8))
        for g in range(8):
            far = levels[np.abs(levels - a[p, g]) >= 10]
            a[p, g + 8] = far[np.random.randint(len(far))]
    return np.exp2(a.ravel()).repeat(32)


BF16 = ml_dtypes.bfloat16


def bf(x):
    return np.asarray(x, np.float32).astype(BF16)


def f64(x):
    return np.asarray(x).astype(np.float64)


E2M1 = np.array([0.0, 0.5, 1.0, 1.5, 2.0, 3.0, 4.0, 6.0, -0.0, -0.5, -1.0, -1.5, -2.0, -3.0, -4.0, -6.0])


def pack_weight(w, fmt):
    k, n = w.shape
    w = f64(bf(w)).reshape(k // 32, 32, n)
    amax = np.abs(w).max(1)
    if fmt == "e4m3":
        byte = np.frexp(amax)[1] - 1 + 127 - 7
    else:
        mant, ex = np.frexp(amax / 6.0)
        byte = np.where(mant > 0.5, ex, ex - 1) + 127
    byte = np.clip(np.where(amax > 0, byte, 1), 1, 254)
    scaled = (w * np.exp2(127.0 - byte)[:, None, :]).reshape(k, n).astype(np.float32)
    by_word = np.ascontiguousarray(scaled.reshape(k // 512, 128, 4, n).transpose(0, 1, 3, 2))
    if fmt == "e4m3":
        words = by_word.astype(ml_dtypes.float8_e4m3fn).view(np.uint8)
    else:
        c = by_word.astype(ml_dtypes.float4_e2m1fn).view(np.uint8) & 0xF
        words = c[..., 0::2] | (c[..., 1::2] << 4)
    return np.ascontiguousarray(words), np.ascontiguousarray(byte.astype(np.uint8).reshape(k // 512, 16, n))


def unpack_weight(words, scales, fmt):
    g, p, n, _ = words.shape
    if fmt == "e4m3":
        vals = np.ascontiguousarray(words).view(ml_dtypes.float8_e4m3fn).astype(np.float64)
    else:
        nib = np.empty((g, p, n, 4), np.uint8)
        nib[..., 0::2] = words & 0xF
        nib[..., 1::2] = words >> 4
        vals = E2M1[nib]
    vals = vals * np.repeat(np.exp2(scales.astype(np.float64) - 127.0), 8, axis=1)[..., None]
    return vals.transpose(0, 1, 3, 2).reshape(g * 512, n)
def pack4(w):
    words, scales = pack_weight(w, "e2m1")
    return words.reshape(words.shape[0], 128, -1), scales


def unpack4(words, scales):
    return unpack_weight(words.reshape(words.shape[0], 128, -1, 2), scales, "e2m1")


def planes(Y):
    n, m = Y.shape
    b = f64(bf(Y)).reshape(n // 32, 32, m)
    amax = np.abs(b).max(1)
    byte = np.clip(np.where(amax > 0, np.frexp(amax)[1] - 1 + 127 - 7, 1), 1, 254)
    codes = (b * np.exp2(127.0 - byte)[:, None, :]).reshape(n, m).astype(np.float32).astype(ml_dtypes.float8_e4m3fn).view(np.uint8)
    words = codes.reshape(n // 512, 128, 4, m).transpose(0, 1, 3, 2)
    return np.ascontiguousarray(words), np.ascontiguousarray(byte.astype(np.uint8).reshape(n // 512, 16, m))


S, R, K, F, N = 8, 128, 1024, 1536, 1024

def setup_inputs():
    s = mx_kscale(K)
    t = mx_kscale(F)
    u = np.random.randn(K, S * R) * s[:, None]
    u_words, u_scales = pack_weight(u, "e4m3")
    w1 = np.random.randn(K, F) / np.sqrt(K) / s[:, None]
    w1_words, w1_scales = pack4(w1)
    state_scale = bf((1.0 + 0.3 * np.random.randn(S, F)) * t[None, :])
    size = np.exp(0.8 * np.random.randn(N))
    w2 = bf(np.random.randn(F, N) / np.sqrt(F) * size[None, :] / t[:, None])
    state_bias = bf(0.4 * np.random.randn(S, N) * size[None, :])
    return {"u_words": u_words, "u_scales": u_scales,
            "w1_words": w1_words, "w1_scales": w1_scales,
            "state_scale": state_scale, "w2": w2, "state_bias": state_bias}

def reference(u_words, u_scales, w1_words, w1_scales, state_scale, w2, state_bias):
    U = unpack_weight(u_words, u_scales, "e4m3")
    W1 = unpack4(w1_words, w1_scales)
    h = U.T @ W1
    e = np.maximum(h, 0.0) + (np.exp(np.minimum(h, 0.0)) - 1.0)
    z = (e.reshape(S, R, F) * f64(state_scale)[:, None, :]).reshape(S * R, F)
    m = mxq(z, 1, "e4m3") @ mxq(f64(w2), 0, "e4m3")
    y = m.reshape(S, R, N) + f64(state_bias)[:, None, :]
    Y = y.reshape(S * R, N).T
    words, scales = planes(Y)
    return y, words, scales

@@ -1,0 +1,310 @@
+from contextlib import ExitStack
+
+import concourse.mybir as mybir
+from concourse.masks import make_identity
+
+S, R, K, F, N = 8, 128, 1024, 1536, 1024
+FLOPS = 2 * S * R * F * (K + N)
+
+F32 = mybir.dt.float32
+BF16 = mybir.dt.bfloat16
+I32 = mybir.dt.int32
+U32 = mybir.dt.uint32
+U8 = mybir.dt.uint8
+FP8X4 = mybir.dt.float8_e4m3fn_x4
+FP4X4 = mybir.dt.float4_e2m1fn_x4
+ALU = mybir.AluOpType
+ACT = mybir.ActivationFunctionType
+
+P = 128
+KG = K // 512
+FG = F // 512
+NH = N // 512
+UNITS = S * FG
+U_LOADS = [(0, 1), (1, 4), (4, 8)]
+HALF_AT = {8: (0, 0), 9: (1, 0), 11: (2, 0), 14: (3, 0), 17: (4, 0), 18: (0, 1), 19: (1, 1), 20: (5, 0),
+           21: (2, 1), 22: (3, 1), 23: (6, 0), 24: (4, 1), 25: (5, 1), 26: (7, 0), 27: (6, 1), 28: (7, 1)}
+LAST_STEP = 32
+
+
+def tile_state_scaled_utility_mixer_h2_kernel(
+    tc, u_words, u_scales, w1_words, w1_scales, state_scale, w2, state_bias, out_0, out_1, out_2
+):
+    nc = tc.nc
+    with ExitStack() as ctx:
+        keep = ctx.enter_context(tc.tile_pool(name="keep", bufs=1))
+        work = ctx.enter_context(tc.tile_pool(name="work", bufs=2))
+        psum = ctx.enter_context(tc.psum_pool(name="psum", bufs=1))
+        ctx.enter_context(tc.manual_schedule())
+
+        w1s_raw = keep.tile([P, KG, F], U8, align_bytes=64)
+        u_sc = keep.tile([P, KG, S * R], U8, align_bytes=64)
+        nc.vector.memset(w1s_raw[:].bitcast(I32), 0)
+        nc.vector.memset(u_sc[:].bitcast(I32), 0)
+        s_rows = keep.tile([P, 4, P], F32)
+        nc.vector.memset(s_rows[:], 0.0)
+        warm = keep.tile([P, 8], F32)
+        nc.scalar.activation(out=warm[:, 0:1], in_=s_rows[:, 0, 0:1], func=ACT.Exp)
+
+        w1_view = w1_words.rearrange("g p b -> p g b")
+        u_view = u_words.rearrange("g p n t -> p g (n t)")
+        w1_first = keep.tile([P, KG, 1024], U8, align_bytes=64)
+        w1_rest = keep.tile([P, KG, 2048], U8, align_bytes=64)
+        u_tiles = []
+        for a, b in U_LOADS:
+            u_tiles.append(keep.tile([P, KG, (b - a) * R], U32, align_bytes=64, name="u%d" % a))
+
+        def load_u(n):
+            a, b = U_LOADS[n]
+            nc.sync.dma_start(out=u_tiles[n][:].bitcast(I32), in_=u_view[:, :, 4 * R * a : 4 * R * b].bitcast(I32))
+
+        def load_scale_rows(queue, tile, dram, q):
+            queue.dma_start(
+                out=tile[32 * q : 32 * q + 4, :, :].bitcast(I32),
+                in_=dram[:, 4 * q : 4 * q + 4, :].rearrange("g r n -> r g n").bitcast(I32),
+            )
+
+        w2_raw = []
+        for g in range(FG):
+            w2_raw.append(keep.tile([P, 4, N], BF16, name="w2raw%d" % g))
+
+        def load_w2(g):
+            rows = w2[512 * g : 512 * (g + 1), :].rearrange("(j t c) n -> c j t n", t=4, c=4)
+            for c in range(4):
+                nc.sync.dma_start(out=w2_raw[g][c:P:4, :, :], in_=rows[c])
+
+        bias = []
+        for b in range(2):
+            bias.append(keep.tile([P, 4 * N], BF16, name="bias%d" % b))
+
+        def load_bias(b):
+            row = state_bias[4 * b : 4 * b + 4, :].rearrange("s n -> (s n)")
+            nc.sync.dma_start(out=bias[b][:], in_=row.partition_broadcast(P))
+
+        s_raw = keep.tile([P, 512], BF16)
+        nc.gpsimd.dma_start(out=s_raw[0:UNITS, :], in_=state_scale.rearrange("s (g f) -> (s g) f", g=FG))
+        nc.sync.dma_start(out=w1_first[:].bitcast(I32), in_=w1_view[:, :, 0:1024].bitcast(I32))
+        load_u(0)
+        for q in range(4):
+            load_scale_rows(nc.sync, w1s_raw, w1_scales, q)
+        for q in range(4):
+            load_scale_rows(nc.sync, u_sc, u_scales, q)
+        nc.sync.dma_start(out=w1_rest[:].bitcast(I32), in_=w1_view[:, :, 1024:3072].bitcast(I32))
+        load_w2(0)
+        load_u(1)
+        load_w2(1)
+        load_u(2)
+        load_w2(2)
+        load_bias(0)
+        load_bias(1)
+
+        ident = keep.tile([P, P], F32)
+        make_identity(nc, ident[:])
+
+        w1c = []
+        w1s = []
+        for g in range(FG):
+            w1c.append(keep.tile([P, KG, 4, 2 * P], U8, align_bytes=64, name="w1c%d" % g))
+            w1s.append(keep.tile([P, KG, 4, P], U8, align_bytes=64, name="w1s%d" % g))
+
+        def sort_w1(g):
+            raw = w1_first[:] if g == 0 else w1_rest[:, :, 1024 * (g - 1) : 1024 * g]
+            nc.vector.tensor_copy(
+                out=w1c[g][:].bitcast(I32).rearrange("p k t (j w) -> p k t j w", w=2),
+                in_=raw.bitcast(I32).rearrange("p k (j t w) -> p k t j w", t=4, w=2),
+            )
+            nc.vector.tensor_copy(
+                out=w1s[g][:].bitcast(I32),
+                in_=w1s_raw[:, :, 512 * g : 512 * (g + 1)].bitcast(I32).rearrange("p k (j t) -> p k t j", t=4),
+            )
+
+        t = {}
+
+        def first_product(k):
+            i, g = divmod(k, FG)
+            h = psum.tile([P, 4, R], F32, tag="h", bufs=4, name="h")
+            t["h", k] = h
+            n = [a <= i < b for a, b in U_LOADS].index(True)
+            c0 = (i - U_LOADS[n][0]) * R
+            for slot in range(4):
+                for kg in range(KG):
+                    nc.tensor.matmul_mx(
+                        out=h[:, slot, :],
+                        lhsT=w1c[g][:, kg, slot, :].bitcast(FP4X4),
+                        lhsT_scale=w1s[g][:, kg, slot, :],
+                        rhs=u_tiles[n][:, kg, c0 : c0 + R].bitcast(FP8X4),
+                        rhs_scale=u_sc[:, kg, i * R : (i + 1) * R],
+                        start=(kg == 0),
+                        stop=(kg == KG - 1),
+                    )
+
+        def neg_part(k):
+            x = work.tile([P, R, 4], F32, tag="x", bufs=2, name="x")
+            t["x", k] = x
+            nc.scalar.activation(out=x[:], in_=t["h", k][:].rearrange("p t r -> p r t"), func=ACT.Relu, scale=-1.0)
+
+        def exp_part(k):
+            ex = work.tile([P, R, 4], F32, tag="ex", bufs=3, name="ex")
+            t["ex", k] = ex
+            nc.scalar.activation(out=ex[:], in_=t["x", k][:], func=ACT.Exp, scale=-1.0)
+
+        def elu(k):
+            e = work.tile([P, R, 4], F32, tag="e", bufs=3, name="e")
+            t["e", k] = e
+            nc.vector.scalar_tensor_tensor(
+                out=e[:], in0=t["ex", k][:], scalar=1.0, in1=t["h", k][:].rearrange("p t r -> p r t"),
+                op0=ALU.subtract, op1=ALU.max,
+            )
+
+        def scale_unit(k):
+            i, g = divmod(k, FG)
+            if g == 0:
+                t["z", i] = work.tile([P, FG, R, 4], BF16, tag="z", bufs=2, align_bytes=64, name="z")
+            nc.vector.tensor_tensor(
+                out=t["z", i][:, g, :, :], in0=t["e", k][:],
+                in1=s_ps[:, k : k + 1, :].to_broadcast([P, R, 4]), op=ALU.mult,
+            )
+
+        z_codes = keep.tile([P, S, FG * R], U32, align_bytes=64)
+        z_sc = keep.tile([P, S, FG * R], U8, align_bytes=64)
+
+        def quant_z(i, g0, g1):
+            nc.vector.quantize_mx(
+                out=z_codes[:, i, g0 * R : g1 * R].bitcast(FP8X4), scales=z_sc[:, i, g0 * R : g1 * R],
+                in_=t["z", i][:, g0:g1, :, :].rearrange("p g r t -> p (g r t)"),
+            )
+
+        w2_codes = keep.tile([P, NH * FG, 512], U32, align_bytes=64)
+        w2_sc = keep.tile([P, NH * FG, 512], U8, align_bytes=64)
+
+        def group_w2(c):
+            h, g = divmod(c, FG)
+            wi = work.tile([P, 512, 4], BF16, tag="wi", bufs=1, align_bytes=64, name="wi")
+            t["wi", c] = wi
+            nc.gpsimd.tensor_scalar(
+                out=wi[:], in0=w2_raw[g][:, :, 512 * h : 512 * (h + 1)].rearrange("p t n -> p n t"),
+                scalar1=1.0, scalar2=0.0, op0=ALU.mult, op1=ALU.add,
+            )
+
+        def quant_w2(c):
+            nc.vector.quantize_mx(
+                out=w2_codes[:, c, :].bitcast(FP8X4), scales=w2_sc[:, c, :],
+                in_=t["wi", c][:].rearrange("p n t -> p (n t)"),
+            )
+
+        def second_product(i, h):
+            m = psum.tile([P, 512], F32, tag="m", bufs=2, name="m")
+            t["m", i, h] = m
+            for g in range(FG):
+                nc.tensor.matmul_mx(
+                    out=m[:],
+                    lhsT=z_codes[:, i, g * R : (g + 1) * R].bitcast(FP8X4), lhsT_scale=z_sc[:, i, g * R : (g + 1) * R],
+                    rhs=w2_codes[:, h * FG + g, :].bitcast(FP8X4), rhs_scale=w2_sc[:, h * FG + g, :],
+                    start=(g == 0), stop=(g == FG - 1),
+                )
+
+        def add_bias(i, h):
+            y = work.tile([P, 512], F32, tag="y", bufs=4, name="y")
+            t["y", i, h] = y
+            c0 = (i % 4) * N + 512 * h
+            nc.vector.tensor_tensor(out=y[:], in0=t["m", i, h][:], in1=bias[i // 4][:, c0 : c0 + 512], op=ALU.add)
+            nc.sync.dma_start(out=out_0[i, :, 512 * h : 512 * (h + 1)], in_=y[:])
+
+        def round_y(i, h):
+            yb = work.tile([P, 512], BF16, tag="yb", bufs=2, name="yb")
+            t["yb", i, h] = yb
+            nc.scalar.copy(
+                out=yb[:].rearrange("r (u p e) -> r u p e", u=2, e=2),
+                in_=t["y", i, h][:].rearrange("r (p u e) -> r u p e", u=2, e=2),
+            )
+
+        def turn_y(i, h):
+            yt = psum.tile([P, 2, R], F32, tag="yt", bufs=1, name="yt")
+            t["yt", i, h] = yt
+            words = t["yb", i, h][:].bitcast(F32)
+            for u in range(2):
+                nc.tensor.transpose(yt[:, u, :], words[:, u * P : (u + 1) * P], ident[:])
+
+        def group_y(i, h):
+            yg = work.tile([P, 512], BF16, tag="yg", bufs=5, align_bytes=64, name="yg")
+            t["yg", i, h] = yg
+            nc.scalar.copy(
+                out=yg[:].bitcast(F32).rearrange("p (r u) -> p r u", u=2),
+                in_=t["yt", i, h][:].rearrange("p u r -> p r u"),
+            )
+
+        y_codes = keep.tile([P, NH, S * R], U32, align_bytes=64)
+        y_sc = keep.tile([P, NH, S * R], U8, align_bytes=64)
+        words_out = out_1.rearrange("g p m t -> g p (m t)")
+
+        def quant_y(i, h):
+            nc.vector.quantize_mx(
+                out=y_codes[:, h, i * R : (i + 1) * R].bitcast(FP8X4), scales=y_sc[:, h, i * R : (i + 1) * R],
+                in_=t["yg", i, h][:],
+            )
+            if i % 2 == 1:
+                nc.sync.dma_start(
+                    out=words_out[h, :, 4 * R * (i - 1) : 4 * R * (i + 1)].bitcast(I32),
+                    in_=y_codes[:, h, (i - 1) * R : (i + 1) * R].bitcast(I32),
+                )
+
+        sort_w1(0)
+        first_product(0)
+        nc.vector.tensor_copy(
+            out=s_rows[0:UNITS, :, :].rearrange("a t (j c) -> a t j c", c=4),
+            in_=s_raw[0:UNITS, :].rearrange("a (j t c) -> a t j c", t=4, c=4),
+        )
+        s_ps = psum.tile([P, P, 4], F32, tag="s", bufs=1, name="s_ps")
+        for slot in range(4):
+            nc.tensor.transpose(s_ps[:, :, slot], s_rows[:, slot, :], ident[:])
+        neg_part(0)
+        exp_part(0)
+        sort_w1(1)
+        sort_w1(2)
+        first_product(1)
+        group_w2(0)
+
+        grouped = []
+        for k in range(LAST_STEP + 1):
+            if k + 2 < UNITS:
+                first_product(k + 2)
+            if k - 3 in HALF_AT:
+                turn_y(*HALF_AT[k - 3])
+            if k in HALF_AT:
+                second_product(*HALF_AT[k])
+            if k + 1 < UNITS:
+                neg_part(k + 1)
+            if k < UNITS:
+                elu(k)
+            if k - 1 in HALF_AT:
+                add_bias(*HALF_AT[k - 1])
+            if k - 2 in HALF_AT:
+                round_y(*HALF_AT[k - 2])
+            if k + 1 < UNITS:
+                exp_part(k + 1)
+            if k % FG == 1 or k > UNITS:
+                i = (k - 4) // FG
+                with_z = k % FG == 1 and 0 <= i < S
+                if with_z:
+                    quant_z(i, 0, 2)
+                    quant_z(i, 2, 3)
+                for half in grouped:
+                    quant_y(*half)
+                grouped = []
+                c = k // FG
+                if k % FG == 1 and c < NH * FG:
+                    quant_w2(c)
+                    if c + 1 < NH * FG:
+                        group_w2(c + 1)
+            if k - 3 in HALF_AT:
+                group_y(*HALF_AT[k - 3])
+                grouped.append(HALF_AT[k - 3])
+            if 0 <= k - 1 < UNITS:
+                scale_unit(k - 1)
+
+        for q in range(4):
+            queue = nc.sync if q % 2 == 0 else nc.scalar
+            queue.dma_start(
+                out=out_2[:, 4 * q : 4 * q + 4, :].rearrange("g r m -> r g m").bitcast(I32),
+                in_=y_sc[32 * q : 32 * q + 4, :, :].bitcast(I32),
+            )

@@ -17,14 +17,42 @@ ALU = mybir.AluOpType
 ACT = mybir.ActivationFunctionType
 
 P = 128
-KG = K // 512
-FG = F // 512
-NH = N // 512
+PASS = 512
+KG = K // PASS
+FG = F // PASS
+NH = N // PASS
 UNITS = S * FG
+CHUNKS = NH * FG
 U_LOADS = [(0, 1), (1, 4), (4, 8)]
-HALF_AT = {8: (0, 0), 9: (1, 0), 11: (2, 0), 14: (3, 0), 17: (4, 0), 18: (0, 1), 19: (1, 1), 20: (5, 0),
-           21: (2, 1), 22: (3, 1), 23: (6, 0), 24: (4, 1), 25: (5, 1), 26: (7, 0), 27: (6, 1), 28: (7, 1)}
-LAST_STEP = 32
+BIAS_STATES = 4
+POOL_UNITS = 2
+
+
+def quantise_step(n):
+    return FG * n + 1
+
+
+def plan_halves():
+    todo = [(i, h) for i in range(S) for h in range(NH)]
+    plan = {}
+    step = 0
+    while todo:
+        ready = [(i, h) for i, h in todo if step > max(quantise_step(i + 1), quantise_step(FG * h + FG - 1))]
+        if ready:
+            plan[step] = ready[0]
+            todo.remove(ready[0])
+        step = step + 1
+    return plan
+
+
+def plan_turns(half_at):
+    first_dense = quantise_step(CHUNKS - 1) + 1
+    plan = {}
+    for step, half in half_at.items():
+        waits_for_partner = step >= first_dense and half[0] < S - 1 and (step - first_dense) % 2 == 0
+        at = step + 3 + (1 if waits_for_partner else 0)
+        plan[at] = plan.get(at, ()) + (half,)
+    return plan
 
 
 def tile_state_scaled_utility_mixer_h2_kernel(
@@ -37,210 +65,226 @@ def tile_state_scaled_utility_mixer_h2_kernel(
         psum = ctx.enter_context(tc.psum_pool(name="psum", bufs=1))
         ctx.enter_context(tc.manual_schedule())
 
-        w1s_raw = keep.tile([P, KG, F], U8, align_bytes=64)
+        w1_sc_raw = keep.tile([P, KG, F], U8, align_bytes=64)
         u_sc = keep.tile([P, KG, S * R], U8, align_bytes=64)
-        nc.vector.memset(w1s_raw[:].bitcast(I32), 0)
-        nc.vector.memset(u_sc[:].bitcast(I32), 0)
         s_rows = keep.tile([P, 4, P], F32)
+        nc.vector.memset(w1_sc_raw[:].bitcast(I32), 0)
+        nc.vector.memset(u_sc[:].bitcast(I32), 0)
         nc.vector.memset(s_rows[:], 0.0)
-        warm = keep.tile([P, 8], F32)
-        nc.scalar.activation(out=warm[:, 0:1], in_=s_rows[:, 0, 0:1], func=ACT.Exp)
 
         w1_view = w1_words.rearrange("g p b -> p g b")
         u_view = u_words.rearrange("g p n t -> p g (n t)")
-        w1_first = keep.tile([P, KG, 1024], U8, align_bytes=64)
-        w1_rest = keep.tile([P, KG, 2048], U8, align_bytes=64)
-        u_tiles = []
-        for a, b in U_LOADS:
-            u_tiles.append(keep.tile([P, KG, (b - a) * R], U32, align_bytes=64, name="u%d" % a))
+        w1_first = keep.tile([P, KG, 2 * PASS], U8, align_bytes=64)
+        w1_rest = keep.tile([P, KG, 2 * (F - PASS)], U8, align_bytes=64)
+        u_codes = [keep.tile([P, KG, (b - a) * R], U32, align_bytes=64, name="u%d" % a) for a, b in U_LOADS]
+        w2_raw = [keep.tile([P, 4, N], BF16, name="w2raw%d" % g) for g in range(FG)]
+        bias = [keep.tile([P, BIAS_STATES * N], BF16, name="bias%d" % b) for b in range(S // BIAS_STATES)]
+        s_raw = keep.tile([P, PASS], BF16)
 
         def load_u(n):
             a, b = U_LOADS[n]
-            nc.sync.dma_start(out=u_tiles[n][:].bitcast(I32), in_=u_view[:, :, 4 * R * a : 4 * R * b].bitcast(I32))
+            nc.sync.dma_start(out=u_codes[n][:].bitcast(I32), in_=u_view[:, :, 4 * R * a : 4 * R * b].bitcast(I32))
 
-        def load_scale_rows(queue, tile, dram, q):
-            queue.dma_start(
-                out=tile[32 * q : 32 * q + 4, :, :].bitcast(I32),
-                in_=dram[:, 4 * q : 4 * q + 4, :].rearrange("g r n -> r g n").bitcast(I32),
-            )
-
-        w2_raw = []
-        for g in range(FG):
-            w2_raw.append(keep.tile([P, 4, N], BF16, name="w2raw%d" % g))
+        def load_scale_rows(plane, rows):
+            for q in range(4):
+                nc.sync.dma_start(
+                    out=plane[32 * q : 32 * q + 4, :, :].bitcast(I32),
+                    in_=rows[:, 4 * q : 4 * q + 4, :].rearrange("g r n -> r g n").bitcast(I32),
+                )
 
         def load_w2(g):
-            rows = w2[512 * g : 512 * (g + 1), :].rearrange("(j t c) n -> c j t n", t=4, c=4)
+            rows = w2[PASS * g : PASS * (g + 1), :].rearrange("(j t c) n -> c j t n", t=4, c=4)
             for c in range(4):
                 nc.sync.dma_start(out=w2_raw[g][c:P:4, :, :], in_=rows[c])
 
-        bias = []
-        for b in range(2):
-            bias.append(keep.tile([P, 4 * N], BF16, name="bias%d" % b))
-
         def load_bias(b):
-            row = state_bias[4 * b : 4 * b + 4, :].rearrange("s n -> (s n)")
+            row = state_bias[BIAS_STATES * b : BIAS_STATES * (b + 1), :].rearrange("s n -> (s n)")
             nc.sync.dma_start(out=bias[b][:], in_=row.partition_broadcast(P))
 
-        s_raw = keep.tile([P, 512], BF16)
         nc.gpsimd.dma_start(out=s_raw[0:UNITS, :], in_=state_scale.rearrange("s (g f) -> (s g) f", g=FG))
-        nc.sync.dma_start(out=w1_first[:].bitcast(I32), in_=w1_view[:, :, 0:1024].bitcast(I32))
+        nc.sync.dma_start(out=w1_first[:].bitcast(I32), in_=w1_view[:, :, 0 : 2 * PASS].bitcast(I32))
         load_u(0)
-        for q in range(4):
-            load_scale_rows(nc.sync, w1s_raw, w1_scales, q)
-        for q in range(4):
-            load_scale_rows(nc.sync, u_sc, u_scales, q)
-        nc.sync.dma_start(out=w1_rest[:].bitcast(I32), in_=w1_view[:, :, 1024:3072].bitcast(I32))
+        load_scale_rows(w1_sc_raw, w1_scales)
+        load_scale_rows(u_sc, u_scales)
+        nc.sync.dma_start(out=w1_rest[:].bitcast(I32), in_=w1_view[:, :, 2 * PASS : 2 * F].bitcast(I32))
         load_w2(0)
         load_u(1)
         load_w2(1)
-        load_u(2)
         load_w2(2)
-        load_bias(0)
-        load_bias(1)
+        load_u(2)
+        for b in range(S // BIAS_STATES):
+            load_bias(b)
 
         ident = keep.tile([P, P], F32)
         make_identity(nc, ident[:])
 
-        w1c = []
-        w1s = []
-        for g in range(FG):
-            w1c.append(keep.tile([P, KG, 4, 2 * P], U8, align_bytes=64, name="w1c%d" % g))
-            w1s.append(keep.tile([P, KG, 4, P], U8, align_bytes=64, name="w1s%d" % g))
+        w1_codes = [keep.tile([P, KG, 4, 2 * P], U8, align_bytes=64, name="w1c%d" % g) for g in range(FG)]
+        w1_sc = [keep.tile([P, KG, 4, P], U8, align_bytes=64, name="w1s%d" % g) for g in range(FG)]
+        z_codes = keep.tile([P, S, FG * R], U32, align_bytes=64)
+        z_sc = keep.tile([P, S, FG * R], U8, align_bytes=64)
+        w2_codes = keep.tile([P, CHUNKS, PASS], U32, align_bytes=64)
+        w2_sc = keep.tile([P, CHUNKS, PASS], U8, align_bytes=64)
+        y_codes = keep.tile([P, NH, S * R], U32, align_bytes=64)
+        y_sc = keep.tile([P, NH, S * R], U8, align_bytes=64)
+        s_psum = psum.tile([P, P, 4], F32, tag="s", bufs=1)
+        s_sbuf = keep.tile([P, UNITS, 4], F32)
+        words_out = out_1.rearrange("g p m t -> g p (m t)")
+        live = {}
 
         def sort_w1(g):
-            raw = w1_first[:] if g == 0 else w1_rest[:, :, 1024 * (g - 1) : 1024 * g]
+            raw = w1_first[:] if g == 0 else w1_rest[:, :, 2 * PASS * (g - 1) : 2 * PASS * g]
             nc.vector.tensor_copy(
-                out=w1c[g][:].bitcast(I32).rearrange("p k t (j w) -> p k t j w", w=2),
+                out=w1_codes[g][:].bitcast(I32).rearrange("p k t (j w) -> p k t j w", w=2),
                 in_=raw.bitcast(I32).rearrange("p k (j t w) -> p k t j w", t=4, w=2),
             )
             nc.vector.tensor_copy(
-                out=w1s[g][:].bitcast(I32),
-                in_=w1s_raw[:, :, 512 * g : 512 * (g + 1)].bitcast(I32).rearrange("p k (j t) -> p k t j", t=4),
+                out=w1_sc[g][:].bitcast(I32),
+                in_=w1_sc_raw[:, :, PASS * g : PASS * (g + 1)].bitcast(I32).rearrange("p k (j t) -> p k t j", t=4),
             )
 
-        t = {}
+        def sort_scale():
+            nc.vector.tensor_copy(
+                out=s_rows[0:UNITS, :, :].rearrange("k t (j c) -> k t j c", c=4),
+                in_=s_raw[0:UNITS, :].rearrange("k (j t c) -> k t j c", t=4, c=4),
+            )
+
+        def turn_scale():
+            for t in range(4):
+                nc.tensor.transpose(s_psum[:, :, t], s_rows[:, t, :], ident[:])
+
+        def copy_scale():
+            nc.scalar.copy(out=s_sbuf[:], in_=s_psum[:, 0:UNITS, :])
 
         def first_product(k):
             i, g = divmod(k, FG)
             h = psum.tile([P, 4, R], F32, tag="h", bufs=4, name="h")
-            t["h", k] = h
+            live["h", k] = h[:].rearrange("p t r -> p r t")
             n = [a <= i < b for a, b in U_LOADS].index(True)
             c0 = (i - U_LOADS[n][0]) * R
-            for slot in range(4):
+            for t in range(4):
                 for kg in range(KG):
                     nc.tensor.matmul_mx(
-                        out=h[:, slot, :],
-                        lhsT=w1c[g][:, kg, slot, :].bitcast(FP4X4),
-                        lhsT_scale=w1s[g][:, kg, slot, :],
-                        rhs=u_tiles[n][:, kg, c0 : c0 + R].bitcast(FP8X4),
+                        out=h[:, t, :],
+                        lhsT=w1_codes[g][:, kg, t, :].bitcast(FP4X4),
+                        lhsT_scale=w1_sc[g][:, kg, t, :],
+                        rhs=u_codes[n][:, kg, c0 : c0 + R].bitcast(FP8X4),
                         rhs_scale=u_sc[:, kg, i * R : (i + 1) * R],
                         start=(kg == 0),
                         stop=(kg == KG - 1),
                     )
 
         def neg_part(k):
-            x = work.tile([P, R, 4], F32, tag="x", bufs=2, name="x")
-            t["x", k] = x
-            nc.scalar.activation(out=x[:], in_=t["h", k][:].rearrange("p t r -> p r t"), func=ACT.Relu, scale=-1.0)
+            x = work.tile([P, R, 4], F32, tag="x", bufs=3, name="x")
+            live["x", k] = x
+            nc.scalar.activation(out=x[:], in_=live["h", k], func=ACT.Relu, scale=-1.0)
 
         def exp_part(k):
             ex = work.tile([P, R, 4], F32, tag="ex", bufs=3, name="ex")
-            t["ex", k] = ex
-            nc.scalar.activation(out=ex[:], in_=t["x", k][:], func=ACT.Exp, scale=-1.0)
+            live["ex", k] = ex
+            nc.scalar.activation(out=ex[:], in_=live["x", k][:], func=ACT.Exp, scale=-1.0)
 
         def elu(k):
-            e = work.tile([P, R, 4], F32, tag="e", bufs=3, name="e")
-            t["e", k] = e
+            e = work.tile([P, R, 4], F32, tag="e", bufs=5, name="e")
+            live["e", k] = e
             nc.vector.scalar_tensor_tensor(
-                out=e[:], in0=t["ex", k][:], scalar=1.0, in1=t["h", k][:].rearrange("p t r -> p r t"),
-                op0=ALU.subtract, op1=ALU.max,
+                out=e[:], in0=live["ex", k][:], scalar=1.0, in1=live["h", k], op0=ALU.subtract, op1=ALU.max
             )
+
+        def on_pool(k):
+            return k // FG >= CHUNKS - 1 and k % FG < POOL_UNITS
 
         def scale_unit(k):
             i, g = divmod(k, FG)
             if g == 0:
-                t["z", i] = work.tile([P, FG, R, 4], BF16, tag="z", bufs=2, align_bytes=64, name="z")
-            nc.vector.tensor_tensor(
-                out=t["z", i][:, g, :, :], in0=t["e", k][:],
-                in1=s_ps[:, k : k + 1, :].to_broadcast([P, R, 4]), op=ALU.mult,
+                live["z", i] = work.tile([P, FG, R, 4], BF16, tag="z", bufs=1, align_bytes=64, name="z")
+            engine, table = (nc.gpsimd, s_sbuf) if on_pool(k) else (nc.vector, s_psum)
+            engine.tensor_tensor(
+                out=live["z", i][:, g, :, :],
+                in0=live["e", k][:],
+                in1=table[:, k : k + 1, :].to_broadcast([P, R, 4]),
+                op=ALU.mult,
             )
-
-        z_codes = keep.tile([P, S, FG * R], U32, align_bytes=64)
-        z_sc = keep.tile([P, S, FG * R], U8, align_bytes=64)
 
         def quant_z(i, g0, g1):
             nc.vector.quantize_mx(
-                out=z_codes[:, i, g0 * R : g1 * R].bitcast(FP8X4), scales=z_sc[:, i, g0 * R : g1 * R],
-                in_=t["z", i][:, g0:g1, :, :].rearrange("p g r t -> p (g r t)"),
+                out=z_codes[:, i, g0 * R : g1 * R].bitcast(FP8X4),
+                scales=z_sc[:, i, g0 * R : g1 * R],
+                in_=live["z", i][:, g0:g1, :, :].rearrange("p g r t -> p (g r t)"),
             )
-
-        w2_codes = keep.tile([P, NH * FG, 512], U32, align_bytes=64)
-        w2_sc = keep.tile([P, NH * FG, 512], U8, align_bytes=64)
 
         def group_w2(c):
             h, g = divmod(c, FG)
-            wi = work.tile([P, 512, 4], BF16, tag="wi", bufs=1, align_bytes=64, name="wi")
-            t["wi", c] = wi
+            wi = work.tile([P, PASS, 4], BF16, tag="wi", bufs=1, align_bytes=64, name="wi")
+            live["wi", c] = wi
             nc.gpsimd.tensor_scalar(
-                out=wi[:], in0=w2_raw[g][:, :, 512 * h : 512 * (h + 1)].rearrange("p t n -> p n t"),
-                scalar1=1.0, scalar2=0.0, op0=ALU.mult, op1=ALU.add,
+                out=wi[:],
+                in0=w2_raw[g][:, :, PASS * h : PASS * (h + 1)].rearrange("p t n -> p n t"),
+                scalar1=1.0,
+                scalar2=0.0,
+                op0=ALU.mult,
+                op1=ALU.add,
             )
 
         def quant_w2(c):
             nc.vector.quantize_mx(
-                out=w2_codes[:, c, :].bitcast(FP8X4), scales=w2_sc[:, c, :],
-                in_=t["wi", c][:].rearrange("p n t -> p (n t)"),
+                out=w2_codes[:, c, :].bitcast(FP8X4),
+                scales=w2_sc[:, c, :],
+                in_=live["wi", c][:].rearrange("p n t -> p (n t)"),
             )
 
         def second_product(i, h):
-            m = psum.tile([P, 512], F32, tag="m", bufs=2, name="m")
-            t["m", i, h] = m
+            m = psum.tile([P, PASS], F32, tag="m", bufs=2, name="m")
+            live["m", i, h] = m
             for g in range(FG):
                 nc.tensor.matmul_mx(
                     out=m[:],
-                    lhsT=z_codes[:, i, g * R : (g + 1) * R].bitcast(FP8X4), lhsT_scale=z_sc[:, i, g * R : (g + 1) * R],
-                    rhs=w2_codes[:, h * FG + g, :].bitcast(FP8X4), rhs_scale=w2_sc[:, h * FG + g, :],
-                    start=(g == 0), stop=(g == FG - 1),
+                    lhsT=z_codes[:, i, g * R : (g + 1) * R].bitcast(FP8X4),
+                    lhsT_scale=z_sc[:, i, g * R : (g + 1) * R],
+                    rhs=w2_codes[:, FG * h + g, :].bitcast(FP8X4),
+                    rhs_scale=w2_sc[:, FG * h + g, :],
+                    start=(g == 0),
+                    stop=(g == FG - 1),
                 )
 
         def add_bias(i, h):
-            y = work.tile([P, 512], F32, tag="y", bufs=4, name="y")
-            t["y", i, h] = y
-            c0 = (i % 4) * N + 512 * h
-            nc.vector.tensor_tensor(out=y[:], in0=t["m", i, h][:], in1=bias[i // 4][:, c0 : c0 + 512], op=ALU.add)
-            nc.sync.dma_start(out=out_0[i, :, 512 * h : 512 * (h + 1)], in_=y[:])
+            y = work.tile([P, PASS], F32, tag="y", bufs=6, name="y")
+            live["y", i, h] = y
+            c0 = (i % BIAS_STATES) * N + PASS * h
+            nc.vector.tensor_tensor(
+                out=y[:], in0=live["m", i, h][:], in1=bias[i // BIAS_STATES][:, c0 : c0 + PASS], op=ALU.add
+            )
+            nc.sync.dma_start(out=out_0[i, :, PASS * h : PASS * (h + 1)], in_=y[:])
 
         def round_y(i, h):
-            yb = work.tile([P, 512], BF16, tag="yb", bufs=2, name="yb")
-            t["yb", i, h] = yb
+            yb = work.tile([P, PASS], BF16, tag="yb", bufs=4, name="yb")
+            live["yb", i, h] = yb
             nc.scalar.copy(
                 out=yb[:].rearrange("r (u p e) -> r u p e", u=2, e=2),
-                in_=t["y", i, h][:].rearrange("r (p u e) -> r u p e", u=2, e=2),
+                in_=live["y", i, h][:].rearrange("r (p u e) -> r u p e", u=2, e=2),
             )
 
-        def turn_y(i, h):
-            yt = psum.tile([P, 2, R], F32, tag="yt", bufs=1, name="yt")
-            t["yt", i, h] = yt
-            words = t["yb", i, h][:].bitcast(F32)
-            for u in range(2):
-                nc.tensor.transpose(yt[:, u, :], words[:, u * P : (u + 1) * P], ident[:])
+        def turn_y(halves):
+            yt = psum.tile([P, len(halves), 2, R], F32, tag="yt", bufs=1, name="yt")
+            live["yt", halves] = yt
+            for n, (i, h) in enumerate(halves):
+                pairs = live["yb", i, h][:].bitcast(F32)
+                for u in range(2):
+                    nc.tensor.transpose(yt[:, n, u, :], pairs[:, u * P : (u + 1) * P], ident[:])
 
-        def group_y(i, h):
-            yg = work.tile([P, 512], BF16, tag="yg", bufs=5, align_bytes=64, name="yg")
-            t["yg", i, h] = yg
+        def group_y(halves):
+            yg = work.tile([P, len(halves), PASS], BF16, tag="yg", bufs=4, align_bytes=64, name="yg")
+            for n, (i, h) in enumerate(halves):
+                live["yg", i, h] = yg[:, n, :]
             nc.scalar.copy(
-                out=yg[:].bitcast(F32).rearrange("p (r u) -> p r u", u=2),
-                in_=t["yt", i, h][:].rearrange("p u r -> p r u"),
+                out=yg[:].bitcast(F32).rearrange("p n (r u) -> p n r u", u=2),
+                in_=live["yt", halves][:].rearrange("p n u r -> p n r u"),
             )
-
-        y_codes = keep.tile([P, NH, S * R], U32, align_bytes=64)
-        y_sc = keep.tile([P, NH, S * R], U8, align_bytes=64)
-        words_out = out_1.rearrange("g p m t -> g p (m t)")
 
         def quant_y(i, h):
             nc.vector.quantize_mx(
-                out=y_codes[:, h, i * R : (i + 1) * R].bitcast(FP8X4), scales=y_sc[:, h, i * R : (i + 1) * R],
-                in_=t["yg", i, h][:],
+                out=y_codes[:, h, i * R : (i + 1) * R].bitcast(FP8X4),
+                scales=y_sc[:, h, i * R : (i + 1) * R],
+                in_=live["yg", i, h],
             )
             if i % 2 == 1:
                 nc.sync.dma_start(
@@ -250,56 +294,61 @@ def tile_state_scaled_utility_mixer_h2_kernel(
 
         sort_w1(0)
         first_product(0)
-        nc.vector.tensor_copy(
-            out=s_rows[0:UNITS, :, :].rearrange("a t (j c) -> a t j c", c=4),
-            in_=s_raw[0:UNITS, :].rearrange("a (j t c) -> a t j c", t=4, c=4),
-        )
-        s_ps = psum.tile([P, P, 4], F32, tag="s", bufs=1, name="s_ps")
-        for slot in range(4):
-            nc.tensor.transpose(s_ps[:, :, slot], s_rows[:, slot, :], ident[:])
+        sort_scale()
         neg_part(0)
         exp_part(0)
         sort_w1(1)
         sort_w1(2)
         first_product(1)
+        neg_part(1)
+        exp_part(1)
+        first_product(2)
+        turn_scale()
         group_w2(0)
 
+        half_at = plan_halves()
+        turn_at = plan_turns(half_at)
         grouped = []
-        for k in range(LAST_STEP + 1):
+        for k in range(max(turn_at) + 2):
+            if k + 3 < UNITS:
+                first_product(k + 3)
+            if k in turn_at:
+                turn_y(turn_at[k])
+            if k in half_at:
+                second_product(*half_at[k])
             if k + 2 < UNITS:
-                first_product(k + 2)
-            if k - 3 in HALF_AT:
-                turn_y(*HALF_AT[k - 3])
-            if k in HALF_AT:
-                second_product(*HALF_AT[k])
-            if k + 1 < UNITS:
-                neg_part(k + 1)
+                neg_part(k + 2)
             if k < UNITS:
                 elu(k)
-            if k - 1 in HALF_AT:
-                add_bias(*HALF_AT[k - 1])
-            if k - 2 in HALF_AT:
-                round_y(*HALF_AT[k - 2])
-            if k + 1 < UNITS:
+            if k - 1 in half_at:
+                add_bias(*half_at[k - 1])
+            if k - 2 in half_at:
+                round_y(*half_at[k - 2])
+            if 2 <= k + 1 < UNITS:
                 exp_part(k + 1)
             if k % FG == 1 or k > UNITS:
-                i = (k - 4) // FG
-                with_z = k % FG == 1 and 0 <= i < S
-                if with_z:
-                    quant_z(i, 0, 2)
-                    quant_z(i, 2, 3)
                 for half in grouped:
                     quant_y(*half)
                 grouped = []
-                c = k // FG
-                if k % FG == 1 and c < NH * FG:
-                    quant_w2(c)
-                    if c + 1 < NH * FG:
-                        group_w2(c + 1)
-            if k - 3 in HALF_AT:
-                group_y(*HALF_AT[k - 3])
-                grouped.append(HALF_AT[k - 3])
-            if 0 <= k - 1 < UNITS:
+            if k % FG == 1:
+                n = k // FG
+                if n == CHUNKS - 1:
+                    quant_w2(n)
+                if 1 <= n <= S:
+                    quant_z(n - 1, 0, 2)
+                    quant_z(n - 1, 2, FG)
+                if n < CHUNKS - 1:
+                    quant_w2(n)
+                    group_w2(n + 1)
+                for unit in (k - 1, k):
+                    if unit < UNITS and on_pool(unit):
+                        scale_unit(unit)
+            if k == FG:
+                copy_scale()
+            if k in turn_at:
+                group_y(turn_at[k])
+                grouped.extend(turn_at[k])
+            if 1 <= k <= UNITS and not on_pool(k - 1):
                 scale_unit(k - 1)
 
         for q in range(4):

@@ -23,9 +23,13 @@ FG = F // PASS
 NH = N // PASS
 UNITS = S * FG
 CHUNKS = NH * FG
-U_LOADS = [(0, 1), (1, 4), (4, 8)]
+U_LOADS = [(0, 2), (2, 4), (4, 8)]
 BIAS_STATES = 4
 POOL_UNITS = 2
+
+
+def unit_of(k):
+    return (k % 2, k // 2) if k < 2 * FG else divmod(k, FG)
 
 
 def quantise_step(n):
@@ -37,7 +41,7 @@ def plan_halves():
     plan = {}
     step = 0
     while todo:
-        ready = [(i, h) for i, h in todo if step > max(quantise_step(i + 1), quantise_step(FG * h + FG - 1))]
+        ready = [(i, h) for i, h in todo if step > max(quantise_step(max(i, 1) + 1), quantise_step(FG * h + FG - 1))]
         if ready:
             plan[step] = ready[0]
             todo.remove(ready[0])
@@ -74,46 +78,55 @@ def tile_state_scaled_utility_mixer_h2_kernel(
 
         w1_view = w1_words.rearrange("g p b -> p g b")
         u_view = u_words.rearrange("g p n t -> p g (n t)")
-        w1_first = keep.tile([P, KG, 2 * PASS], U8, align_bytes=64)
-        w1_rest = keep.tile([P, KG, 2 * (F - PASS)], U8, align_bytes=64)
+        w1_raw = [keep.tile([P, KG, 2 * PASS], U8, align_bytes=64, name="w1raw%d" % g) for g in range(FG - 1)]
+        w1_raw.append(work.tile([P, KG, 2 * PASS], U8, tag="wi", bufs=1, align_bytes=64, name="w1last"))
         u_codes = [keep.tile([P, KG, (b - a) * R], U32, align_bytes=64, name="u%d" % a) for a, b in U_LOADS]
-        w2_raw = [keep.tile([P, 4, N], BF16, name="w2raw%d" % g) for g in range(FG)]
+        w2_raw = [keep.tile([P, 4, PASS], BF16, name="w2raw%d" % c) for c in range(CHUNKS)]
         bias = [keep.tile([P, BIAS_STATES * N], BF16, name="bias%d" % b) for b in range(S // BIAS_STATES)]
         s_raw = keep.tile([P, PASS], BF16)
+
+        def load_w1(g):
+            cols = slice(2 * PASS * g, 2 * PASS * (g + 1))
+            nc.sync.dma_start(out=w1_raw[g][:].bitcast(I32), in_=w1_view[:, :, cols].bitcast(I32))
 
         def load_u(n):
             a, b = U_LOADS[n]
             nc.sync.dma_start(out=u_codes[n][:].bitcast(I32), in_=u_view[:, :, 4 * R * a : 4 * R * b].bitcast(I32))
 
         def load_scale_rows(plane, rows):
-            for q in range(4):
+            for q in (0, 2, 1, 3):
                 nc.sync.dma_start(
                     out=plane[32 * q : 32 * q + 4, :, :].bitcast(I32),
                     in_=rows[:, 4 * q : 4 * q + 4, :].rearrange("g r n -> r g n").bitcast(I32),
                 )
 
-        def load_w2(g):
-            rows = w2[PASS * g : PASS * (g + 1), :].rearrange("(j t c) n -> c j t n", t=4, c=4)
+        def load_w2(chunk):
+            h, g = divmod(chunk, FG)
+            rows = w2[PASS * g : PASS * (g + 1), PASS * h : PASS * (h + 1)].rearrange("(j t c) n -> c j t n", t=4, c=4)
             for c in range(4):
-                nc.sync.dma_start(out=w2_raw[g][c:P:4, :, :], in_=rows[c])
+                nc.sync.dma_start(out=w2_raw[chunk][c:P:4, :, :], in_=rows[c])
 
         def load_bias(b):
             row = state_bias[BIAS_STATES * b : BIAS_STATES * (b + 1), :].rearrange("s n -> (s n)")
             nc.sync.dma_start(out=bias[b][:], in_=row.partition_broadcast(P))
 
         nc.gpsimd.dma_start(out=s_raw[0:UNITS, :], in_=state_scale.rearrange("s (g f) -> (s g) f", g=FG))
-        nc.sync.dma_start(out=w1_first[:].bitcast(I32), in_=w1_view[:, :, 0 : 2 * PASS].bitcast(I32))
+        load_w1(0)
         load_u(0)
         load_scale_rows(w1_sc_raw, w1_scales)
         load_scale_rows(u_sc, u_scales)
-        nc.sync.dma_start(out=w1_rest[:].bitcast(I32), in_=w1_view[:, :, 2 * PASS : 2 * F].bitcast(I32))
+        load_w1(1)
+        load_w1(2)
         load_w2(0)
-        load_u(1)
         load_w2(1)
+        load_u(1)
         load_w2(2)
         load_u(2)
-        for b in range(S // BIAS_STATES):
-            load_bias(b)
+        load_w2(3)
+        load_bias(0)
+        load_w2(4)
+        load_w2(5)
+        load_bias(1)
 
         ident = keep.tile([P, P], F32)
         make_identity(nc, ident[:])
@@ -132,10 +145,9 @@ def tile_state_scaled_utility_mixer_h2_kernel(
         live = {}
 
         def sort_w1(g):
-            raw = w1_first[:] if g == 0 else w1_rest[:, :, 2 * PASS * (g - 1) : 2 * PASS * g]
             nc.vector.tensor_copy(
                 out=w1_codes[g][:].bitcast(I32).rearrange("p k t (j w) -> p k t j w", w=2),
-                in_=raw.bitcast(I32).rearrange("p k (j t w) -> p k t j w", t=4, w=2),
+                in_=w1_raw[g][:].bitcast(I32).rearrange("p k (j t w) -> p k t j w", t=4, w=2),
             )
             nc.vector.tensor_copy(
                 out=w1_sc[g][:].bitcast(I32),
@@ -155,8 +167,13 @@ def tile_state_scaled_utility_mixer_h2_kernel(
         def copy_scale():
             nc.scalar.copy(out=s_sbuf[:], in_=s_psum[:, 0:UNITS, :])
 
+        def bank(shape, tag, bufs, late):
+            if late:
+                return psum.tile(shape, F32, tag="h", bufs=4, name=tag)
+            return psum.tile(shape, F32, tag=tag, bufs=bufs, name=tag)
+
         def first_product(k):
-            i, g = divmod(k, FG)
+            i, g = unit_of(k)
             h = psum.tile([P, 4, R], F32, tag="h", bufs=4, name="h")
             live["h", k] = h[:].rearrange("p t r -> p r t")
             n = [a <= i < b for a, b in U_LOADS].index(True)
@@ -194,14 +211,16 @@ def tile_state_scaled_utility_mixer_h2_kernel(
             return k // FG >= CHUNKS - 1 and k % FG < POOL_UNITS
 
         def scale_unit(k):
-            i, g = divmod(k, FG)
+            i, g = unit_of(k)
             if g == 0:
-                live["z", i] = work.tile([P, FG, R, 4], BF16, tag="z", bufs=1, align_bytes=64, name="z")
+                live["z", i] = work.tile(
+                    [P, FG, R, 4], BF16, tag="z" if i else "z0", bufs=1, align_bytes=64, name="z"
+                )
             engine, table = (nc.gpsimd, s_sbuf) if on_pool(k) else (nc.vector, s_psum)
             engine.tensor_tensor(
                 out=live["z", i][:, g, :, :],
                 in0=live["e", k][:],
-                in1=table[:, k : k + 1, :].to_broadcast([P, R, 4]),
+                in1=table[:, FG * i + g : FG * i + g + 1, :].to_broadcast([P, R, 4]),
                 op=ALU.mult,
             )
 
@@ -213,12 +232,11 @@ def tile_state_scaled_utility_mixer_h2_kernel(
             )
 
         def group_w2(c):
-            h, g = divmod(c, FG)
             wi = work.tile([P, PASS, 4], BF16, tag="wi", bufs=1, align_bytes=64, name="wi")
             live["wi", c] = wi
             nc.gpsimd.tensor_scalar(
                 out=wi[:],
-                in0=w2_raw[g][:, :, PASS * h : PASS * (h + 1)].rearrange("p t n -> p n t"),
+                in0=w2_raw[c][:].rearrange("p t n -> p n t"),
                 scalar1=1.0,
                 scalar2=0.0,
                 op0=ALU.mult,
@@ -232,8 +250,8 @@ def tile_state_scaled_utility_mixer_h2_kernel(
                 in_=live["wi", c][:].rearrange("p n t -> p (n t)"),
             )
 
-        def second_product(i, h):
-            m = psum.tile([P, PASS], F32, tag="m", bufs=2, name="m")
+        def second_product(i, h, late):
+            m = bank([P, PASS], "m", 2, late)
             live["m", i, h] = m
             for g in range(FG):
                 nc.tensor.matmul_mx(
@@ -263,8 +281,8 @@ def tile_state_scaled_utility_mixer_h2_kernel(
                 in_=live["y", i, h][:].rearrange("r (p u e) -> r u p e", u=2, e=2),
             )
 
-        def turn_y(halves):
-            yt = psum.tile([P, len(halves), 2, R], F32, tag="yt", bufs=1, name="yt")
+        def turn_y(halves, late):
+            yt = bank([P, len(halves), 2, R], "yt", 1, late)
             live["yt", halves] = yt
             for n, (i, h) in enumerate(halves):
                 pairs = live["yb", i, h][:].bitcast(F32)
@@ -292,18 +310,26 @@ def tile_state_scaled_utility_mixer_h2_kernel(
                     in_=y_codes[:, h, (i - 1) * R : (i + 1) * R].bitcast(I32),
                 )
 
+        def store_scales(i0, i1):
+            for q in range(4):
+                queue = nc.sync if q % 2 == 0 else nc.scalar
+                queue.dma_start(
+                    out=out_2[:, 4 * q : 4 * q + 4, i0 * R : i1 * R].rearrange("g r m -> r g m").bitcast(I32),
+                    in_=y_sc[32 * q : 32 * q + 4, :, i0 * R : i1 * R].bitcast(I32),
+                )
+
         sort_w1(0)
         first_product(0)
         sort_scale()
         neg_part(0)
         exp_part(0)
-        sort_w1(1)
-        sort_w1(2)
         first_product(1)
         neg_part(1)
         exp_part(1)
-        first_product(2)
         turn_scale()
+        sort_w1(1)
+        sort_w1(2)
+        first_product(2)
         group_w2(0)
 
         half_at = plan_halves()
@@ -313,9 +339,9 @@ def tile_state_scaled_utility_mixer_h2_kernel(
             if k + 3 < UNITS:
                 first_product(k + 3)
             if k in turn_at:
-                turn_y(turn_at[k])
+                turn_y(turn_at[k], k >= UNITS)
             if k in half_at:
-                second_product(*half_at[k])
+                second_product(*half_at[k], False)
             if k + 2 < UNITS:
                 neg_part(k + 2)
             if k < UNITS:
@@ -326,17 +352,25 @@ def tile_state_scaled_utility_mixer_h2_kernel(
                 round_y(*half_at[k - 2])
             if 2 <= k + 1 < UNITS:
                 exp_part(k + 1)
+            if k == 0:
+                scale_unit(k)
+            if k == quantise_step(S):
+                quant_z(S - 1, 0, 2)
+                quant_z(S - 1, 2, FG)
             if k % FG == 1 or k > UNITS:
                 for half in grouped:
                     quant_y(*half)
+                    if half == (S - 3, NH - 1):
+                        store_scales(0, S - 2)
                 grouped = []
             if k % FG == 1:
                 n = k // FG
                 if n == CHUNKS - 1:
                     quant_w2(n)
-                if 1 <= n <= S:
-                    quant_z(n - 1, 0, 2)
-                    quant_z(n - 1, 2, FG)
+                for i in range(S - 1):
+                    if max(i, 1) + 1 == n:
+                        quant_z(i, 0, 2)
+                        quant_z(i, 2, FG)
                 if n < CHUNKS - 1:
                     quant_w2(n)
                     group_w2(n + 1)
@@ -348,12 +382,7 @@ def tile_state_scaled_utility_mixer_h2_kernel(
             if k in turn_at:
                 group_y(turn_at[k])
                 grouped.extend(turn_at[k])
-            if 1 <= k <= UNITS and not on_pool(k - 1):
+            if 2 <= k <= UNITS and not on_pool(k - 1):
                 scale_unit(k - 1)
 
-        for q in range(4):
-            queue = nc.sync if q % 2 == 0 else nc.scalar
-            queue.dma_start(
-                out=out_2[:, 4 * q : 4 * q + 4, :].rearrange("g r m -> r g m").bitcast(I32),
-                in_=y_sc[32 * q : 32 * q + 4, :, :].bitcast(I32),
-            )
+        store_scales(S - 2, S)

@@ -32,8 +32,12 @@ def unit_of(k):
     return (k % 2, k // 2) if k < 2 * FG else divmod(k, FG)
 
 
-def quantise_step(n):
-    return FG * n + 1
+def quantise_step(batch):
+    return FG * batch + 1
+
+
+def z_batch(i):
+    return max(i, 1) + 1
 
 
 def plan_halves():
@@ -41,7 +45,7 @@ def plan_halves():
     plan = {}
     step = 0
     while todo:
-        ready = [(i, h) for i, h in todo if step > max(quantise_step(max(i, 1) + 1), quantise_step(FG * h + FG - 1))]
+        ready = [(i, h) for i, h in todo if step > max(quantise_step(z_batch(i)), quantise_step(FG * h + FG - 1))]
         if ready:
             plan[step] = ready[0]
             todo.remove(ready[0])
@@ -76,12 +80,12 @@ def tile_state_scaled_utility_mixer_h2_kernel(
         nc.vector.memset(u_sc[:].bitcast(I32), 0)
         nc.vector.memset(s_rows[:], 0.0)
 
-        w1_view = w1_words.rearrange("g p b -> p g b")
-        u_view = u_words.rearrange("g p n t -> p g (n t)")
+        w1_view = w1_words.rearrange("kg p b -> p kg b")
+        u_view = u_words.rearrange("kg p row t -> p kg (row t)")
         w1_raw = [keep.tile([P, KG, 2 * PASS], U8, align_bytes=64, name="w1raw%d" % g) for g in range(FG - 1)]
         w1_raw.append(work.tile([P, KG, 2 * PASS], U8, tag="wi", bufs=1, align_bytes=64, name="w1last"))
-        u_codes = [keep.tile([P, KG, (b - a) * R], U32, align_bytes=64, name="u%d" % a) for a, b in U_LOADS]
-        w2_raw = [keep.tile([P, 4, PASS], BF16, name="w2raw%d" % c) for c in range(CHUNKS)]
+        u_codes = [keep.tile([P, KG, (i1 - i0) * R], U32, align_bytes=64, name="u%d" % i0) for i0, i1 in U_LOADS]
+        w2_raw = [keep.tile([P, 4, PASS], BF16, name="w2raw%d" % chunk) for chunk in range(CHUNKS)]
         bias = [keep.tile([P, BIAS_STATES * N], BF16, name="bias%d" % b) for b in range(S // BIAS_STATES)]
         s_raw = keep.tile([P, PASS], BF16)
 
@@ -89,15 +93,16 @@ def tile_state_scaled_utility_mixer_h2_kernel(
             cols = slice(2 * PASS * g, 2 * PASS * (g + 1))
             nc.sync.dma_start(out=w1_raw[g][:].bitcast(I32), in_=w1_view[:, :, cols].bitcast(I32))
 
-        def load_u(n):
-            a, b = U_LOADS[n]
-            nc.sync.dma_start(out=u_codes[n][:].bitcast(I32), in_=u_view[:, :, 4 * R * a : 4 * R * b].bitcast(I32))
+        def load_u(load):
+            i0, i1 = U_LOADS[load]
+            cols = slice(4 * R * i0, 4 * R * i1)
+            nc.sync.dma_start(out=u_codes[load][:].bitcast(I32), in_=u_view[:, :, cols].bitcast(I32))
 
-        def load_scale_rows(plane, rows):
-            for q in (0, 2, 1, 3):
+        def load_scale_rows(tile_sc, rows):
+            for quad in (0, 2, 1, 3):
                 nc.sync.dma_start(
-                    out=plane[32 * q : 32 * q + 4, :, :].bitcast(I32),
-                    in_=rows[:, 4 * q : 4 * q + 4, :].rearrange("g r n -> r g n").bitcast(I32),
+                    out=tile_sc[32 * quad : 32 * quad + 4, :, :].bitcast(I32),
+                    in_=rows[:, 4 * quad : 4 * quad + 4, :].rearrange("kg r col -> r kg col").bitcast(I32),
                 )
 
         def load_w2(chunk):
@@ -141,23 +146,23 @@ def tile_state_scaled_utility_mixer_h2_kernel(
         y_sc = keep.tile([P, NH, S * R], U8, align_bytes=64)
         s_psum = psum.tile([P, P, 4], F32, tag="s", bufs=1)
         s_sbuf = keep.tile([P, UNITS, 4], F32)
-        words_out = out_1.rearrange("g p m t -> g p (m t)")
+        words_out = out_1.rearrange("h p row t -> h p (row t)")
         live = {}
 
         def sort_w1(g):
             nc.vector.tensor_copy(
-                out=w1_codes[g][:].bitcast(I32).rearrange("p k t (j w) -> p k t j w", w=2),
-                in_=w1_raw[g][:].bitcast(I32).rearrange("p k (j t w) -> p k t j w", t=4, w=2),
+                out=w1_codes[g][:].bitcast(I32).rearrange("p kg t (j w) -> p kg t j w", w=2),
+                in_=w1_raw[g][:].bitcast(I32).rearrange("p kg (j t w) -> p kg t j w", t=4, w=2),
             )
             nc.vector.tensor_copy(
                 out=w1_sc[g][:].bitcast(I32),
-                in_=w1_sc_raw[:, :, PASS * g : PASS * (g + 1)].bitcast(I32).rearrange("p k (j t) -> p k t j", t=4),
+                in_=w1_sc_raw[:, :, PASS * g : PASS * (g + 1)].bitcast(I32).rearrange("p kg (j t) -> p kg t j", t=4),
             )
 
         def sort_scale():
             nc.vector.tensor_copy(
-                out=s_rows[0:UNITS, :, :].rearrange("k t (j c) -> k t j c", c=4),
-                in_=s_raw[0:UNITS, :].rearrange("k (j t c) -> k t j c", t=4, c=4),
+                out=s_rows[0:UNITS, :, :].rearrange("row t (j c) -> row t j c", c=4),
+                in_=s_raw[0:UNITS, :].rearrange("row (j t c) -> row t j c", t=4, c=4),
             )
 
         def turn_scale():
@@ -169,22 +174,22 @@ def tile_state_scaled_utility_mixer_h2_kernel(
 
         def bank(shape, tag, bufs, late):
             if late:
-                return psum.tile(shape, F32, tag="h", bufs=4, name=tag)
+                return psum.tile(shape, F32, tag="a", bufs=4, name=tag)
             return psum.tile(shape, F32, tag=tag, bufs=bufs, name=tag)
 
         def first_product(k):
             i, g = unit_of(k)
-            h = psum.tile([P, 4, R], F32, tag="h", bufs=4, name="h")
-            live["h", k] = h[:].rearrange("p t r -> p r t")
-            n = [a <= i < b for a, b in U_LOADS].index(True)
-            c0 = (i - U_LOADS[n][0]) * R
+            a = psum.tile([P, 4, R], F32, tag="a", bufs=4, name="a")
+            live["a", k] = a[:].rearrange("p t r -> p r t")
+            load = [i0 <= i < i1 for i0, i1 in U_LOADS].index(True)
+            col0 = (i - U_LOADS[load][0]) * R
             for t in range(4):
                 for kg in range(KG):
                     nc.tensor.matmul_mx(
-                        out=h[:, t, :],
+                        out=a[:, t, :],
                         lhsT=w1_codes[g][:, kg, t, :].bitcast(FP4X4),
                         lhsT_scale=w1_sc[g][:, kg, t, :],
-                        rhs=u_codes[n][:, kg, c0 : c0 + R].bitcast(FP8X4),
+                        rhs=u_codes[load][:, kg, col0 : col0 + R].bitcast(FP8X4),
                         rhs_scale=u_sc[:, kg, i * R : (i + 1) * R],
                         start=(kg == 0),
                         stop=(kg == KG - 1),
@@ -193,7 +198,7 @@ def tile_state_scaled_utility_mixer_h2_kernel(
         def neg_part(k):
             x = work.tile([P, R, 4], F32, tag="x", bufs=3, name="x")
             live["x", k] = x
-            nc.scalar.activation(out=x[:], in_=live["h", k], func=ACT.Relu, scale=-1.0)
+            nc.scalar.activation(out=x[:], in_=live["a", k], func=ACT.Relu, scale=-1.0)
 
         def exp_part(k):
             ex = work.tile([P, R, 4], F32, tag="ex", bufs=3, name="ex")
@@ -204,7 +209,7 @@ def tile_state_scaled_utility_mixer_h2_kernel(
             e = work.tile([P, R, 4], F32, tag="e", bufs=5, name="e")
             live["e", k] = e
             nc.vector.scalar_tensor_tensor(
-                out=e[:], in0=live["ex", k][:], scalar=1.0, in1=live["h", k], op0=ALU.subtract, op1=ALU.max
+                out=e[:], in0=live["ex", k][:], scalar=1.0, in1=live["a", k], op0=ALU.subtract, op1=ALU.max
             )
 
         def on_pool(k):
@@ -231,23 +236,27 @@ def tile_state_scaled_utility_mixer_h2_kernel(
                 in_=live["z", i][:, g0:g1, :, :].rearrange("p g r t -> p (g r t)"),
             )
 
-        def group_w2(c):
+        def quant_state(i):
+            quant_z(i, 0, 2)
+            quant_z(i, 2, FG)
+
+        def group_w2(chunk):
             wi = work.tile([P, PASS, 4], BF16, tag="wi", bufs=1, align_bytes=64, name="wi")
-            live["wi", c] = wi
+            live["wi", chunk] = wi
             nc.gpsimd.tensor_scalar(
                 out=wi[:],
-                in0=w2_raw[c][:].rearrange("p t n -> p n t"),
+                in0=w2_raw[chunk][:].rearrange("p t n -> p n t"),
                 scalar1=1.0,
                 scalar2=0.0,
                 op0=ALU.mult,
                 op1=ALU.add,
             )
 
-        def quant_w2(c):
+        def quant_w2(chunk):
             nc.vector.quantize_mx(
-                out=w2_codes[:, c, :].bitcast(FP8X4),
-                scales=w2_sc[:, c, :],
-                in_=live["wi", c][:].rearrange("p n t -> p (n t)"),
+                out=w2_codes[:, chunk, :].bitcast(FP8X4),
+                scales=w2_sc[:, chunk, :],
+                in_=live["wi", chunk][:].rearrange("p n t -> p (n t)"),
             )
 
         def second_product(i, h, late):
@@ -267,16 +276,17 @@ def tile_state_scaled_utility_mixer_h2_kernel(
         def add_bias(i, h):
             y = work.tile([P, PASS], F32, tag="y", bufs=6, name="y")
             live["y", i, h] = y
-            c0 = (i % BIAS_STATES) * N + PASS * h
+            col0 = (i % BIAS_STATES) * N + PASS * h
             nc.vector.tensor_tensor(
-                out=y[:], in0=live["m", i, h][:], in1=bias[i // BIAS_STATES][:, c0 : c0 + PASS], op=ALU.add
+                out=y[:], in0=live["m", i, h][:], in1=bias[i // BIAS_STATES][:, col0 : col0 + PASS], op=ALU.add
             )
             nc.sync.dma_start(out=out_0[i, :, PASS * h : PASS * (h + 1)], in_=y[:])
 
-        def round_y(i, h):
+        def round_y(i, h, on_vector):
             yb = work.tile([P, PASS], BF16, tag="yb", bufs=4, name="yb")
             live["yb", i, h] = yb
-            nc.scalar.copy(
+            copy = nc.vector.tensor_copy if on_vector else nc.scalar.copy
+            copy(
                 out=yb[:].rearrange("r (u p e) -> r u p e", u=2, e=2),
                 in_=live["y", i, h][:].rearrange("r (p u e) -> r u p e", u=2, e=2),
             )
@@ -284,18 +294,18 @@ def tile_state_scaled_utility_mixer_h2_kernel(
         def turn_y(halves, late):
             yt = bank([P, len(halves), 2, R], "yt", 1, late)
             live["yt", halves] = yt
-            for n, (i, h) in enumerate(halves):
+            for slot, (i, h) in enumerate(halves):
                 pairs = live["yb", i, h][:].bitcast(F32)
                 for u in range(2):
-                    nc.tensor.transpose(yt[:, n, u, :], pairs[:, u * P : (u + 1) * P], ident[:])
+                    nc.tensor.transpose(yt[:, slot, u, :], pairs[:, u * P : (u + 1) * P], ident[:])
 
         def group_y(halves):
             yg = work.tile([P, len(halves), PASS], BF16, tag="yg", bufs=4, align_bytes=64, name="yg")
-            for n, (i, h) in enumerate(halves):
-                live["yg", i, h] = yg[:, n, :]
+            for slot, (i, h) in enumerate(halves):
+                live["yg", i, h] = yg[:, slot, :]
             nc.scalar.copy(
-                out=yg[:].bitcast(F32).rearrange("p n (r u) -> p n r u", u=2),
-                in_=live["yt", halves][:].rearrange("p n u r -> p n r u"),
+                out=yg[:].bitcast(F32).rearrange("p slot (r u) -> p slot r u", u=2),
+                in_=live["yt", halves][:].rearrange("p slot u r -> p slot r u"),
             )
 
         def quant_y(i, h):
@@ -310,12 +320,12 @@ def tile_state_scaled_utility_mixer_h2_kernel(
                     in_=y_codes[:, h, (i - 1) * R : (i + 1) * R].bitcast(I32),
                 )
 
-        def store_scales(i0, i1):
-            for q in range(4):
-                queue = nc.sync if q % 2 == 0 else nc.scalar
+        def store_scales(i0, i1, last):
+            for quad in range(4):
+                queue = nc.scalar if last and quad % 2 else nc.sync
                 queue.dma_start(
-                    out=out_2[:, 4 * q : 4 * q + 4, i0 * R : i1 * R].rearrange("g r m -> r g m").bitcast(I32),
-                    in_=y_sc[32 * q : 32 * q + 4, :, i0 * R : i1 * R].bitcast(I32),
+                    out=out_2[:, 4 * quad : 4 * quad + 4, i0 * R : i1 * R].rearrange("h r row -> r h row").bitcast(I32),
+                    in_=y_sc[32 * quad : 32 * quad + 4, :, i0 * R : i1 * R].bitcast(I32),
                 )
 
         sort_w1(0)
@@ -341,7 +351,7 @@ def tile_state_scaled_utility_mixer_h2_kernel(
             if k in turn_at:
                 turn_y(turn_at[k], k >= UNITS)
             if k in half_at:
-                second_product(*half_at[k], False)
+                second_product(*half_at[k], k >= UNITS)
             if k + 2 < UNITS:
                 neg_part(k + 2)
             if k < UNITS:
@@ -349,31 +359,29 @@ def tile_state_scaled_utility_mixer_h2_kernel(
             if k - 1 in half_at:
                 add_bias(*half_at[k - 1])
             if k - 2 in half_at:
-                round_y(*half_at[k - 2])
+                round_y(*half_at[k - 2], half_at[k - 2] == (S - 1, NH - 1))
             if 2 <= k + 1 < UNITS:
                 exp_part(k + 1)
             if k == 0:
                 scale_unit(k)
-            if k == quantise_step(S):
-                quant_z(S - 1, 0, 2)
-                quant_z(S - 1, 2, FG)
+            if k == quantise_step(z_batch(S - 1)):
+                quant_state(S - 1)
             if k % FG == 1 or k > UNITS:
                 for half in grouped:
                     quant_y(*half)
                     if half == (S - 3, NH - 1):
-                        store_scales(0, S - 2)
+                        store_scales(0, S - 2, False)
                 grouped = []
             if k % FG == 1:
-                n = k // FG
-                if n == CHUNKS - 1:
-                    quant_w2(n)
+                batch = k // FG
+                if batch == CHUNKS - 1:
+                    quant_w2(batch)
                 for i in range(S - 1):
-                    if max(i, 1) + 1 == n:
-                        quant_z(i, 0, 2)
-                        quant_z(i, 2, FG)
-                if n < CHUNKS - 1:
-                    quant_w2(n)
-                    group_w2(n + 1)
+                    if z_batch(i) == batch:
+                        quant_state(i)
+                if batch < CHUNKS - 1:
+                    quant_w2(batch)
+                    group_w2(batch + 1)
                 for unit in (k - 1, k):
                     if unit < UNITS and on_pool(unit):
                         scale_unit(unit)
@@ -385,4 +393,4 @@ def tile_state_scaled_utility_mixer_h2_kernel(
             if 2 <= k <= UNITS and not on_pool(k - 1):
                 scale_unit(k - 1)
 
-        store_scales(S - 2, S)
+        store_scales(S - 2, S, True)

from contextlib import ExitStack

import concourse.mybir as mybir
from concourse.masks import make_identity

S, R, K, F, N = 8, 128, 1024, 1536, 1024
FLOPS = 2 * S * R * F * (K + N)

F32 = mybir.dt.float32
BF16 = mybir.dt.bfloat16
I32 = mybir.dt.int32
U32 = mybir.dt.uint32
U8 = mybir.dt.uint8
FP8X4 = mybir.dt.float8_e4m3fn_x4
FP4X4 = mybir.dt.float4_e2m1fn_x4
ALU = mybir.AluOpType
ACT = mybir.ActivationFunctionType

P = 128
PASS = 512
KG = K // PASS
FG = F // PASS
NH = N // PASS
UNITS = S * FG
CHUNKS = NH * FG
U_LOADS = [(0, 2), (2, 4), (4, 8)]
BIAS_STATES = 4
POOL_UNITS = 2


def unit_of(k):
    return (k % 2, k // 2) if k < 2 * FG else divmod(k, FG)


def quantise_step(batch):
    return FG * batch + 1


def z_batch(i):
    return max(i, 1) + 1


def plan_halves():
    todo = [(i, h) for i in range(S) for h in range(NH)]
    plan = {}
    step = 0
    while todo:
        ready = [(i, h) for i, h in todo if step > max(quantise_step(z_batch(i)), quantise_step(FG * h + FG - 1))]
        if ready:
            plan[step] = ready[0]
            todo.remove(ready[0])
        step = step + 1
    return plan


def plan_turns(half_at):
    first_dense = quantise_step(CHUNKS - 1) + 1
    plan = {}
    for step, half in half_at.items():
        waits_for_partner = step >= first_dense and half[0] < S - 1 and (step - first_dense) % 2 == 0
        at = step + 3 + (1 if waits_for_partner else 0)
        plan[at] = plan.get(at, ()) + (half,)
    return plan


def tile_state_scaled_utility_mixer_h2_kernel(
    tc, u_words, u_scales, w1_words, w1_scales, state_scale, w2, state_bias, out_0, out_1, out_2
):
    nc = tc.nc
    with ExitStack() as ctx:
        keep = ctx.enter_context(tc.tile_pool(name="keep", bufs=1))
        work = ctx.enter_context(tc.tile_pool(name="work", bufs=2))
        psum = ctx.enter_context(tc.psum_pool(name="psum", bufs=1))
        ctx.enter_context(tc.manual_schedule())

        w1_sc_raw = keep.tile([P, KG, F], U8, align_bytes=64)
        u_sc = keep.tile([P, KG, S * R], U8, align_bytes=64)
        s_rows = keep.tile([P, 4, P], F32)
        nc.vector.memset(w1_sc_raw[:].bitcast(I32), 0)
        nc.vector.memset(u_sc[:].bitcast(I32), 0)
        nc.vector.memset(s_rows[:], 0.0)

        w1_view = w1_words.rearrange("kg p b -> p kg b")
        u_view = u_words.rearrange("kg p row t -> p kg (row t)")
        w1_raw = [keep.tile([P, KG, 2 * PASS], U8, align_bytes=64, name="w1raw%d" % g) for g in range(FG - 1)]
        w1_raw.append(work.tile([P, KG, 2 * PASS], U8, tag="wi", bufs=1, align_bytes=64, name="w1last"))
        u_codes = [keep.tile([P, KG, (i1 - i0) * R], U32, align_bytes=64, name="u%d" % i0) for i0, i1 in U_LOADS]
        w2_raw = [keep.tile([P, 4, PASS], BF16, name="w2raw%d" % chunk) for chunk in range(CHUNKS)]
        bias = [keep.tile([P, BIAS_STATES * N], BF16, name="bias%d" % b) for b in range(S // BIAS_STATES)]
        s_raw = keep.tile([P, PASS], BF16)

        def load_w1(g):
            cols = slice(2 * PASS * g, 2 * PASS * (g + 1))
            nc.sync.dma_start(out=w1_raw[g][:].bitcast(I32), in_=w1_view[:, :, cols].bitcast(I32))

        def load_u(load):
            i0, i1 = U_LOADS[load]
            cols = slice(4 * R * i0, 4 * R * i1)
            nc.sync.dma_start(out=u_codes[load][:].bitcast(I32), in_=u_view[:, :, cols].bitcast(I32))

        def load_scale_rows(tile_sc, rows):
            for quad in (0, 2, 1, 3):
                nc.sync.dma_start(
                    out=tile_sc[32 * quad : 32 * quad + 4, :, :].bitcast(I32),
                    in_=rows[:, 4 * quad : 4 * quad + 4, :].rearrange("kg r col -> r kg col").bitcast(I32),
                )

        def load_w2(chunk):
            h, g = divmod(chunk, FG)
            rows = w2[PASS * g : PASS * (g + 1), PASS * h : PASS * (h + 1)].rearrange("(j t c) n -> c j t n", t=4, c=4)
            for c in range(4):
                nc.sync.dma_start(out=w2_raw[chunk][c:P:4, :, :], in_=rows[c])

        def load_bias(b):
            row = state_bias[BIAS_STATES * b : BIAS_STATES * (b + 1), :].rearrange("s n -> (s n)")
            nc.sync.dma_start(out=bias[b][:], in_=row.partition_broadcast(P))

        nc.gpsimd.dma_start(out=s_raw[0:UNITS, :], in_=state_scale.rearrange("s (g f) -> (s g) f", g=FG))
        load_w1(0)
        load_u(0)
        load_scale_rows(w1_sc_raw, w1_scales)
        load_scale_rows(u_sc, u_scales)
        load_w1(1)
        load_w1(2)
        load_w2(0)
        load_w2(1)
        load_u(1)
        load_w2(2)
        load_u(2)
        load_w2(3)
        load_bias(0)
        load_w2(4)
        load_w2(5)
        load_bias(1)

        ident = keep.tile([P, P], F32)
        make_identity(nc, ident[:])

        w1_codes = [keep.tile([P, KG, 4, 2 * P], U8, align_bytes=64, name="w1c%d" % g) for g in range(FG)]
        w1_sc = [keep.tile([P, KG, 4, P], U8, align_bytes=64, name="w1s%d" % g) for g in range(FG)]
        z_codes = keep.tile([P, S, FG * R], U32, align_bytes=64)
        z_sc = keep.tile([P, S, FG * R], U8, align_bytes=64)
        w2_codes = keep.tile([P, CHUNKS, PASS], U32, align_bytes=64)
        w2_sc = keep.tile([P, CHUNKS, PASS], U8, align_bytes=64)
        y_codes = keep.tile([P, NH, S * R], U32, align_bytes=64)
        y_sc = keep.tile([P, NH, S * R], U8, align_bytes=64)
        s_psum = psum.tile([P, P, 4], F32, tag="s", bufs=1)
        s_sbuf = keep.tile([P, UNITS, 4], F32)
        words_out = out_1.rearrange("h p row t -> h p (row t)")
        live = {}

        def sort_w1(g):
            nc.vector.tensor_copy(
                out=w1_codes[g][:].bitcast(I32).rearrange("p kg t (j w) -> p kg t j w", w=2),
                in_=w1_raw[g][:].bitcast(I32).rearrange("p kg (j t w) -> p kg t j w", t=4, w=2),
            )
            nc.vector.tensor_copy(
                out=w1_sc[g][:].bitcast(I32),
                in_=w1_sc_raw[:, :, PASS * g : PASS * (g + 1)].bitcast(I32).rearrange("p kg (j t) -> p kg t j", t=4),
            )

        def sort_scale():
            nc.vector.tensor_copy(
                out=s_rows[0:UNITS, :, :].rearrange("row t (j c) -> row t j c", c=4),
                in_=s_raw[0:UNITS, :].rearrange("row (j t c) -> row t j c", t=4, c=4),
            )

        def turn_scale():
            for t in range(4):
                nc.tensor.transpose(s_psum[:, :, t], s_rows[:, t, :], ident[:])

        def copy_scale():
            nc.scalar.copy(out=s_sbuf[:], in_=s_psum[:, 0:UNITS, :])

        def bank(shape, tag, bufs, late):
            if late:
                return psum.tile(shape, F32, tag="a", bufs=4, name=tag)
            return psum.tile(shape, F32, tag=tag, bufs=bufs, name=tag)

        def first_product(k):
            i, g = unit_of(k)
            a = psum.tile([P, 4, R], F32, tag="a", bufs=4, name="a")
            live["a", k] = a[:].rearrange("p t r -> p r t")
            load = [i0 <= i < i1 for i0, i1 in U_LOADS].index(True)
            col0 = (i - U_LOADS[load][0]) * R
            for t in range(4):
                for kg in range(KG):
                    nc.tensor.matmul_mx(
                        out=a[:, t, :],
                        lhsT=w1_codes[g][:, kg, t, :].bitcast(FP4X4),
                        lhsT_scale=w1_sc[g][:, kg, t, :],
                        rhs=u_codes[load][:, kg, col0 : col0 + R].bitcast(FP8X4),
                        rhs_scale=u_sc[:, kg, i * R : (i + 1) * R],
                        start=(kg == 0),
                        stop=(kg == KG - 1),
                    )

        def neg_part(k):
            x = work.tile([P, R, 4], F32, tag="x", bufs=3, name="x")
            live["x", k] = x
            nc.scalar.activation(out=x[:], in_=live["a", k], func=ACT.Relu, scale=-1.0)

        def exp_part(k):
            ex = work.tile([P, R, 4], F32, tag="ex", bufs=3, name="ex")
            live["ex", k] = ex
            nc.scalar.activation(out=ex[:], in_=live["x", k][:], func=ACT.Exp, scale=-1.0)

        def elu(k):
            e = work.tile([P, R, 4], F32, tag="e", bufs=5, name="e")
            live["e", k] = e
            nc.vector.scalar_tensor_tensor(
                out=e[:], in0=live["ex", k][:], scalar=1.0, in1=live["a", k], op0=ALU.subtract, op1=ALU.max
            )

        def on_pool(k):
            return k // FG >= CHUNKS - 1 and k % FG < POOL_UNITS

        def scale_unit(k):
            i, g = unit_of(k)
            if g == 0:
                live["z", i] = work.tile(
                    [P, FG, R, 4], BF16, tag="z" if i else "z0", bufs=1, align_bytes=64, name="z"
                )
            engine, table = (nc.gpsimd, s_sbuf) if on_pool(k) else (nc.vector, s_psum)
            engine.tensor_tensor(
                out=live["z", i][:, g, :, :],
                in0=live["e", k][:],
                in1=table[:, FG * i + g : FG * i + g + 1, :].to_broadcast([P, R, 4]),
                op=ALU.mult,
            )

        def quant_z(i, g0, g1):
            nc.vector.quantize_mx(
                out=z_codes[:, i, g0 * R : g1 * R].bitcast(FP8X4),
                scales=z_sc[:, i, g0 * R : g1 * R],
                in_=live["z", i][:, g0:g1, :, :].rearrange("p g r t -> p (g r t)"),
            )

        def quant_state(i):
            quant_z(i, 0, 2)
            quant_z(i, 2, FG)

        def group_w2(chunk):
            wi = work.tile([P, PASS, 4], BF16, tag="wi", bufs=1, align_bytes=64, name="wi")
            live["wi", chunk] = wi
            nc.gpsimd.tensor_scalar(
                out=wi[:],
                in0=w2_raw[chunk][:].rearrange("p t n -> p n t"),
                scalar1=1.0,
                scalar2=0.0,
                op0=ALU.mult,
                op1=ALU.add,
            )

        def quant_w2(chunk):
            nc.vector.quantize_mx(
                out=w2_codes[:, chunk, :].bitcast(FP8X4),
                scales=w2_sc[:, chunk, :],
                in_=live["wi", chunk][:].rearrange("p n t -> p (n t)"),
            )

        def second_product(i, h, late):
            m = bank([P, PASS], "m", 2, late)
            live["m", i, h] = m
            for g in range(FG):
                nc.tensor.matmul_mx(
                    out=m[:],
                    lhsT=z_codes[:, i, g * R : (g + 1) * R].bitcast(FP8X4),
                    lhsT_scale=z_sc[:, i, g * R : (g + 1) * R],
                    rhs=w2_codes[:, FG * h + g, :].bitcast(FP8X4),
                    rhs_scale=w2_sc[:, FG * h + g, :],
                    start=(g == 0),
                    stop=(g == FG - 1),
                )

        def add_bias(i, h):
            y = work.tile([P, PASS], F32, tag="y", bufs=6, name="y")
            live["y", i, h] = y
            col0 = (i % BIAS_STATES) * N + PASS * h
            nc.vector.tensor_tensor(
                out=y[:], in0=live["m", i, h][:], in1=bias[i // BIAS_STATES][:, col0 : col0 + PASS], op=ALU.add
            )
            nc.sync.dma_start(out=out_0[i, :, PASS * h : PASS * (h + 1)], in_=y[:])

        def round_y(i, h, on_vector):
            yb = work.tile([P, PASS], BF16, tag="yb", bufs=4, name="yb")
            live["yb", i, h] = yb
            copy = nc.vector.tensor_copy if on_vector else nc.scalar.copy
            copy(
                out=yb[:].rearrange("r (u p e) -> r u p e", u=2, e=2),
                in_=live["y", i, h][:].rearrange("r (p u e) -> r u p e", u=2, e=2),
            )

        def turn_y(halves, late):
            yt = bank([P, len(halves), 2, R], "yt", 1, late)
            live["yt", halves] = yt
            for slot, (i, h) in enumerate(halves):
                pairs = live["yb", i, h][:].bitcast(F32)
                for u in range(2):
                    nc.tensor.transpose(yt[:, slot, u, :], pairs[:, u * P : (u + 1) * P], ident[:])

        def group_y(halves):
            yg = work.tile([P, len(halves), PASS], BF16, tag="yg", bufs=4, align_bytes=64, name="yg")
            for slot, (i, h) in enumerate(halves):
                live["yg", i, h] = yg[:, slot, :]
            nc.scalar.copy(
                out=yg[:].bitcast(F32).rearrange("p slot (r u) -> p slot r u", u=2),
                in_=live["yt", halves][:].rearrange("p slot u r -> p slot r u"),
            )

        def quant_y(i, h):
            nc.vector.quantize_mx(
                out=y_codes[:, h, i * R : (i + 1) * R].bitcast(FP8X4),
                scales=y_sc[:, h, i * R : (i + 1) * R],
                in_=live["yg", i, h],
            )
            if i % 2 == 1:
                nc.sync.dma_start(
                    out=words_out[h, :, 4 * R * (i - 1) : 4 * R * (i + 1)].bitcast(I32),
                    in_=y_codes[:, h, (i - 1) * R : (i + 1) * R].bitcast(I32),
                )

        def store_scales(i0, i1, last):
            for quad in range(4):
                queue = nc.scalar if last and quad % 2 else nc.sync
                queue.dma_start(
                    out=out_2[:, 4 * quad : 4 * quad + 4, i0 * R : i1 * R].rearrange("h r row -> r h row").bitcast(I32),
                    in_=y_sc[32 * quad : 32 * quad + 4, :, i0 * R : i1 * R].bitcast(I32),
                )

        sort_w1(0)
        first_product(0)
        sort_scale()
        neg_part(0)
        exp_part(0)
        first_product(1)
        neg_part(1)
        exp_part(1)
        turn_scale()
        sort_w1(1)
        sort_w1(2)
        first_product(2)
        group_w2(0)

        half_at = plan_halves()
        turn_at = plan_turns(half_at)
        grouped = []
        for k in range(max(turn_at) + 2):
            if k + 3 < UNITS:
                first_product(k + 3)
            if k in turn_at:
                turn_y(turn_at[k], k >= UNITS)
            if k in half_at:
                second_product(*half_at[k], k >= UNITS)
            if k + 2 < UNITS:
                neg_part(k + 2)
            if k < UNITS:
                elu(k)
            if k - 1 in half_at:
                add_bias(*half_at[k - 1])
            if k - 2 in half_at:
                round_y(*half_at[k - 2], half_at[k - 2] == (S - 1, NH - 1))
            if 2 <= k + 1 < UNITS:
                exp_part(k + 1)
            if k == 0:
                scale_unit(k)
            if k == quantise_step(z_batch(S - 1)):
                quant_state(S - 1)
            if k % FG == 1 or k > UNITS:
                for half in grouped:
                    quant_y(*half)
                    if half == (S - 3, NH - 1):
                        store_scales(0, S - 2, False)
                grouped = []
            if k % FG == 1:
                batch = k // FG
                if batch == CHUNKS - 1:
                    quant_w2(batch)
                for i in range(S - 1):
                    if z_batch(i) == batch:
                        quant_state(i)
                if batch < CHUNKS - 1:
                    quant_w2(batch)
                    group_w2(batch + 1)
                for unit in (k - 1, k):
                    if unit < UNITS and on_pool(unit):
                        scale_unit(unit)
            if k == FG:
                copy_scale()
            if k in turn_at:
                group_y(turn_at[k])
                grouped.extend(turn_at[k])
            if 2 <= k <= UNITS and not on_pool(k - 1):
                scale_unit(k - 1)

        store_scales(S - 2, S, True)
